import numpy as np
import ml_dtypes


def mxq(x, axis, fmt="e4m3"):
    dtype, down = {"e4m3": (ml_dtypes.float8_e4m3fn, 7), "e5m2": (ml_dtypes.float8_e5m2, 14)}[fmt]
    v = np.moveaxis(np.asarray(x, np.float32).astype(ml_dtypes.bfloat16).astype(np.float64), axis, -1)
    blocks = v.reshape(v.shape[:-1] + (-1, 32))
    amax = np.abs(blocks).max(-1, keepdims=True)
    byte = np.maximum(np.where(amax > 0, np.frexp(amax)[1] - 1 + 127, 0) - down, 1)
    scale = np.exp2(byte - 127.0)
    codes = (blocks / scale).astype(np.float32).astype(dtype).astype(np.float64)
    return np.moveaxis((codes * scale).reshape(v.shape), -1, axis)


WIDE = False


def mx_kscale(k):
    if not WIDE:
        return np.ones(k)
    levels = np.array([10, -10, 5, -5, 0])
    if k % 512:
        return np.exp2(np.random.permutation(np.resize(levels, k // 32))).repeat(32)
    a = np.empty((k // 512, 16))
    for p in range(k // 512):
        a[p, :8] = np.random.permutation(np.resize(levels, 8))
        for g in range(8):
            far = levels[np.abs(levels - a[p, g]) >= 10]
            a[p, g + 8] = far[np.random.randint(len(far))]
    return np.exp2(a.ravel()).repeat(32)


def f64(x):
    return np.asarray(x).astype(np.float64)


def striped(idx):
    return np.tile(idx.reshape(-1, 16).T, (8, 1)).astype(np.uint16)


def unstriped(offs):
    return offs[:16].T.reshape(-1).astype(np.int64)


E2M1 = np.array([0.0, 0.5, 1.0, 1.5, 2.0, 3.0, 4.0, 6.0, -0.0, -0.5, -1.0, -1.5, -2.0, -3.0, -4.0, -6.0])


def pack_weight(w, fmt):
    k, n = w.shape
    w = f64(np.asarray(w, np.float32).astype(ml_dtypes.bfloat16)).reshape(k // 32, 32, n)
    amax = np.abs(w).max(1)
    if fmt == "e4m3":
        byte = np.frexp(amax)[1] - 1 + 127 - 7
    else:
        mant, ex = np.frexp(amax / 6.0)
        byte = np.where(mant > 0.5, ex, ex - 1) + 127
    byte = np.clip(np.where(amax > 0, byte, 1), 1, 254)
    scaled = (w * np.exp2(127.0 - byte)[:, None, :]).reshape(k, n).astype(np.float32)
    by_word = np.ascontiguousarray(scaled.reshape(k // 512, 128, 4, n).transpose(0, 1, 3, 2))
    if fmt == "e4m3":
        words = by_word.astype(ml_dtypes.float8_e4m3fn).view(np.uint8)
    else:
        c = by_word.astype(ml_dtypes.float4_e2m1fn).view(np.uint8) & 0xF
        words = (c[..., 0::2] | (c[..., 1::2] << 4)).reshape(k // 512, 128, 2 * n)
    return np.ascontiguousarray(words), np.ascontiguousarray(byte.astype(np.uint8).reshape(k // 512, 16, n))


def unpack_weight(words, scales, fmt):
    g, _, n = scales.shape
    words = np.ascontiguousarray(words).reshape(g, 128, n, -1)
    if fmt == "e4m3":
        vals = words.view(ml_dtypes.float8_e4m3fn).astype(np.float64)
    else:
        nib = np.empty((g, 128, n, 4), np.uint8)
        nib[..., 0::2] = words & 0xF
        nib[..., 1::2] = words >> 4
        vals = E2M1[nib]
    vals = vals * np.repeat(np.exp2(scales.astype(np.float64) - 127.0), 8, axis=1)[..., None]
    return vals.transpose(0, 1, 3, 2).reshape(g * 512, n)


def relu2(v):
    return np.maximum(v, 0.0) ** 2


K, T, E, C, H, TOP, COPIES = 512, 768, 5, 256, 512, 3, 576
PAD = 64


def by_expert(wq, xq):
    return np.concatenate([wq[e].T @ xq[:, e * C:(e + 1) * C] for e in range(E)], axis=1)


def setup_inputs():
    n = np.random.standard_normal
    s = mx_kscale(K)
    u = mx_kscale(H)
    left = TOP * T - E * C - COPIES
    deal = np.repeat(np.arange(E + 2), [C] * E + [COPIES, left]).reshape(TOP, T)[:, np.random.permutation(T)]
    deal = np.take_along_axis(deal, np.argsort(np.random.rand(TOP, T), axis=0), axis=0)
    for _ in range(8):
        s_, t_ = np.random.permutation(T).reshape(2, -1); r = np.random.randint(TOP, size=T // 2); x, y = deal[r, s_].copy(), deal[r, t_].copy()
        ok = ~((deal[:, s_] == y).any(0) | (deal[:, t_] == x).any(0)); deal[r[ok], s_[ok]] = y[ok]; deal[r[ok], t_[ok]] = x[ok]
    order = np.lexsort((np.random.rand(TOP * T), deal.reshape(-1)))[:E * C]
    slot_token = order % T
    pos = np.where(deal == E, E * C + np.arange(T), E * C + T + np.arange(T) % PAD).reshape(-1); pos[order] = np.arange(E * C); pos = pos.reshape(TOP, T)
    g = np.random.uniform(0.5, 1.5, (TOP, T)); g = g / g.sum(0)
    xf = n((K, T))
    x = pack_weight(xf * s[:, None], "e4m3")
    w1 = [pack_weight(m, "e4m3") for m in n((E, K, H)) / np.sqrt(K) / s[None, :, None] * u]
    w2 = [pack_weight(m, "e4m3") for m in n((E, H, K)) / np.sqrt(H) / u[None, :, None] ** 2]
    return {
        "x_words": x[0],
        "x_scales": x[1],
        "xr": (xf).astype(np.float32),
        "w1_words": np.stack([m[0] for m in w1]),
        "w1_scales": np.stack([m[1] for m in w1]),
        "w2_words": np.stack([m[0] for m in w2]),
        "w2_scales": np.stack([m[1] for m in w2]),
        "gate": np.stack([np.tile(r, (128, 1)) for r in g]).astype(np.float32),
        "offs": striped(slot_token),
        "pos1": striped(pos[0]),
        "pos2": striped(pos[1]),
        "pos3": striped(pos[2]),
    }


def reference(x_words, x_scales, xr, w1_words, w1_scales, w2_words, w2_scales, gate, offs, pos1, pos2, pos3):
    w1 = np.stack([unpack_weight(w1_words[e], w1_scales[e], "e4m3") for e in range(E)])
    w2 = np.stack([unpack_weight(w2_words[e], w2_scales[e], "e4m3") for e in range(E)])
    idx = unstriped(offs)
    xq = unpack_weight(x_words, x_scales, "e4m3")[:, idx]
    h = relu2(by_expert(w1, xq))
    y = by_expert(w2, mxq(h, 0, "e4m3"))
    y = np.concatenate([y, f64(xr), np.zeros((K, PAD))], axis=1)
    out = sum(f64(gate[r, :1]) * y[:, unstriped(p)] for r, p in enumerate((pos1, pos2, pos3)))
    return out

@@ -1,0 +1,265 @@
+from contextlib import ExitStack
+
+import concourse.mybir as mybir
+from concourse.masks import make_identity
+
+K, T, E, C, H, TOP, PAD = 512, 768, 5, 256, 512, 3, 64
+S = E * C
+W = S + T + PAD
+P = 128
+FLOPS = 2 * S * K * H * 2
+
+F32 = mybir.dt.float32
+BF16 = mybir.dt.bfloat16
+I32 = mybir.dt.int32
+U32 = mybir.dt.uint32
+U16 = mybir.dt.uint16
+U8 = mybir.dt.uint8
+FP8X4 = mybir.dt.float8_e4m3fn_x4
+ACT = mybir.ActivationFunctionType
+ALU = mybir.AluOpType
+
+RELU_ON_VECTOR = [6,7,8,9]
+Y_ON_VECTOR = [1,2]
+TAIL = 256
+
+
+def tile_moe_cpy_mlp_relu2_kernel(
+    tc, x_words, x_scales, xr, w1_words, w1_scales, w2_words, w2_scales, gate, offs, pos1, pos2, pos3, out
+):
+    nc = tc.nc
+    with ExitStack() as ctx:
+        keep = ctx.enter_context(tc.tile_pool(name="keep", bufs=1))
+        ring = ctx.enter_context(tc.tile_pool(name="ring", bufs=2))
+        psum = ctx.enter_context(tc.psum_pool(name="psum", bufs=1))
+
+        def held(shape, dtype, name):
+            return keep.tile(shape, dtype, name=name, align_bytes=64)
+
+        def words(ap):
+            return ap.rearrange("p n t -> p (n t)").bitcast(I32)
+
+        xs = held([P, T], U8, "xs")
+        w1s = held([P, 2 * H], U8, "w1s")
+        w2s = held([P, E * K], U8, "w2s")
+        nc.gpsimd.memset(xs[:].bitcast(I32), 0)
+        nc.gpsimd.memset(w1s[:].bitcast(I32), 0)
+        nc.gpsimd.memset(w2s[:].bitcast(I32), 0)
+        zeros = held([P, PAD], F32, "zeros")
+        nc.gpsimd.memset(zeros[:], 0.0)
+        ident = held([P, P], F32, "ident")
+        make_identity(nc, ident[:])
+
+        slot_list = held([P, S // 16], U16, "slot_list")
+        nc.sync.dma_start(slot_list[:], offs)
+        xw = held([P, T], I32, "xw")
+        nc.sync.dma_start(xw[:], words(x_words[0]))
+        for q in range(4):
+            nc.sync.dma_start(xs[32 * q : 32 * q + 4, :].bitcast(I32), x_scales[0, 4 * q : 4 * q + 4, :].bitcast(I32))
+        w1 = [held([P, H], I32, f"w1_{e}") for e in range(E)]
+        nc.sync.dma_start(w1[0][:], words(w1_words[0, 0]))
+        for q in range(4):
+            nc.sync.dma_start(
+                w1s[32 * q : 32 * q + 16, 0:H].bitcast(I32), w1_scales[0:4, 0, 4 * q : 4 * q + 4, :].bitcast(I32)
+            )
+        for e in range(1, E):
+            nc.sync.dma_start(w1[e][:], words(w1_words[e, 0]))
+        for q in range(4):
+            nc.sync.dma_start(
+                w1s[32 * q : 32 * q + 4, H : 2 * H].bitcast(I32), w1_scales[4, 0, 4 * q : 4 * q + 4, :].bitcast(I32)
+            )
+        for q in range(4):
+            nc.sync.dma_start(
+                w2s[32 * q : 32 * q + 4, :].bitcast(I32).rearrange("j (e n) -> j e n", e=E),
+                w2_scales[:, 0, 4 * q : 4 * q + 4, :].bitcast(I32).rearrange("e j n -> j e n"),
+            )
+        w2 = held([P, E * K], I32, "w2")
+        nc.sync.dma_start(
+            w2[:].rearrange("p (e n) -> p e n", e=E),
+            w2_words[:, 0].rearrange("e p n t -> p e (n t)").bitcast(I32),
+        )
+        win = [held([P, W], F32, f"win_{b}") for b in range(4)]
+        nc.sync.dma_start(win[0][:, S : S + T], xr[0:P, :])
+        back = []
+        for r, lst in enumerate((pos1, pos2, pos3)):
+            t = held([P, T // 16], U16, f"back_{r}")
+            nc.sync.dma_start(t[:], lst)
+            back.append(t)
+        g = held([P, TOP * T], F32, "g")
+        nc.sync.dma_start(g[:].rearrange("p (r t) -> p r t", r=TOP), gate.rearrange("r p t -> p r t"))
+        for b in range(1, 4):
+            nc.sync.dma_start(win[b][:, S : S + T], xr[b * P : (b + 1) * P, :])
+        for b in range(4):
+            nc.scalar.activation(win[b][:, S + T : W], zeros[:], ACT.Relu)
+
+        gw = {}
+        gs = {}
+        w1p = [held([P, H], I32, f"w1p_{e}") for e in range(E)]
+        w1sp = [held([P, H], U8, f"w1sp_{c}") for c in range(2)]
+        hq = [held([P, C], U32, f"hq_{e}") for e in range(E)]
+        hs = [held([P, C], U8, f"hs_{e}") for e in range(E)]
+
+        def gather_words(a, b):
+            t = keep.tile([P, b - a], U32, name="gw", tag="gw", bufs=2, align_bytes=64)
+            nc.vector.tensor_copy(t[:], xw[:].bitcast(U32).indirect(slot_list[:, a // 16 : b // 16]))
+            for c in range(a, b, P):
+                gw[c // P] = t[:, c - a : c - a + P]
+
+        def gather_scales(a, b):
+            t = keep.tile([P, b - a], U8, name="gs", tag="gs", bufs=1, align_bytes=64)
+            nc.vector.tensor_copy(t[:], xs[:].indirect(slot_list[:, a // 16 : b // 16]))
+            for c in range(a, b, P):
+                gs[c // P] = t[:, c - a : c - a + P]
+
+        def permute_words(e):
+            nc.vector.tensor_copy(
+                w1p[e][:].rearrange("p (t c i) -> p c t i", t=4, i=4),
+                w1[e][:].rearrange("p (c i t) -> p c t i", t=4, i=4),
+            )
+
+        def permute_scales(c):
+            nc.vector.tensor_copy(
+                w1sp[c][:].rearrange("p (t m) -> p t m", t=4),
+                w1s[:, c * H : (c + 1) * H].rearrange("p (m t) -> p t m", t=4),
+            )
+
+        rl = {}
+        hb = {}
+
+        def first_layer(u):
+            e, half = divmod(u, 2)
+            bank = psum.tile([P, 4, P], F32, name="bank", tag="bank", bufs=4)
+            row = 4 * (e % 4)
+            for t in range(4):
+                nc.tensor.matmul_mx(
+                    bank[:, t, :],
+                    lhsT=w1p[e][:, t * P : (t + 1) * P].bitcast(FP8X4),
+                    lhsT_scale=w1sp[e // 4][row:P, t * P : (t + 1) * P],
+                    rhs=gw[u].bitcast(FP8X4),
+                    rhs_scale=gs[u],
+                    start=True,
+                    stop=True,
+                )
+            if half == 0:
+                rl[e] = ring.tile([P, 4 * C], F32, name="rl", align_bytes=64)
+                hb[e] = ring.tile([P, 4 * C], BF16, name="hb", align_bytes=64)
+            dst = rl[e][:, half * 4 * P : (half + 1) * 4 * P].rearrange("p (s t) -> p s t", t=4)
+            src = bank[:].rearrange("p t s -> p s t")
+            if u in RELU_ON_VECTOR:
+                nc.vector.tensor_scalar(dst, src, 0.0, None, ALU.max)
+            else:
+                nc.scalar.activation(dst, src, ACT.Relu)
+
+        def square(e, a, b):
+            nc.scalar.activation(hb[e][:, 4 * a : 4 * b], rl[e][:, 4 * a : 4 * b], ACT.Square)
+
+        def quantise(e, a, b):
+            nc.vector.quantize_mx(hq[e][:, a:b].bitcast(FP8X4), hs[e][:, a:b], hb[e][:, 4 * a : 4 * b])
+
+        def second_layer(b, experts, width, on_vector):
+            bank = psum.tile([P, 2 * C], F32, name="ybank", tag="ybank", bufs=2)
+            for j, e in enumerate(experts):
+                for a in range(0, C, width):
+                    nc.tensor.matmul_mx(
+                        bank[:, j * C + a : j * C + a + width],
+                        lhsT=w2[:, e * K + b * P : e * K + (b + 1) * P].bitcast(FP8X4),
+                        lhsT_scale=w2s[:, e * K + b * P : e * K + (b + 1) * P],
+                        rhs=hq[e][:, a : a + width].bitcast(FP8X4),
+                        rhs_scale=hs[e][:, a : a + width],
+                        start=True,
+                        stop=True,
+                    )
+            n = len(experts) * C
+            dst = win[b][:, experts[0] * C : experts[0] * C + n]
+            if on_vector:
+                nc.vector.tensor_copy(dst, bank[:, 0:n])
+            else:
+                nc.scalar.copy(dst, bank[:, 0:n])
+
+        gather_words(0, C)
+        gather_scales(0, C)
+        permute_words(0)
+        gather_words(C, 2 * C)
+        permute_scales(0)
+        first_layer(0)
+        first_layer(1)
+        permute_words(1)
+        permute_words(2)
+        gather_scales(C, 3 * C)
+        square(0, 0, C)
+        first_layer(2)
+        first_layer(3)
+        gather_words(2 * C, 4 * C)
+        quantise(0, 0, C)
+        square(1, 0, C)
+        first_layer(4)
+        first_layer(5)
+        permute_words(3)
+        gather_words(4 * C, S)
+        gather_scales(3 * C, S)
+        quantise(1, 0, C)
+        permute_words(4)
+        permute_scales(1)
+        square(2, 0, C)
+        second_layer(0, (0, 1), C, 0 in Y_ON_VECTOR)
+        first_layer(6)
+        first_layer(7)
+        quantise(2, 0, C)
+        square(3, 0, C)
+        first_layer(8)
+        first_layer(9)
+        quantise(3, 0, C)
+        square(4, 0, P)
+        square(4, P, C)
+        second_layer(0, (2, 3), C, 1 in Y_ON_VECTOR)
+        quantise(4, 0, P)
+        quantise(4, P, C)
+        second_layer(0, (4,), P, 2 in Y_ON_VECTOR)
+
+        def fill(b):
+            for experts in ((0, 1), (2, 3), (4,)):
+                second_layer(b, experts, C, False)
+
+        def weighted(b, r, a, n, tag):
+            prod = ring.tile([P, n], F32, name=tag, tag=tag, align_bytes=64)
+            nc.vector.tensor_tensor(
+                prod[:], win[b][:].indirect(back[r][:, a // 16 : (a + n) // 16]), g[:, r * T + a : r * T + a + n], ALU.mult
+            )
+            return prod
+
+        def add_on_tensor(b, prods, a, t0, n):
+            blocks = n // P
+            turned = psum.tile([P, n], F32, name="turned", tag="bank", bufs=4)
+            for r in range(TOP):
+                for j in range(blocks):
+                    nc.tensor.matmul(
+                        turned[:, j * P : (j + 1) * P],
+                        prods[r][:, a + j * P : a + (j + 1) * P],
+                        ident[:],
+                        start=(r == 0 and j == 0),
+                        stop=(r == TOP - 1 and j == blocks - 1),
+                        is_transpose=True,
+                    )
+            total = ring.tile([P, n], F32, name="total", tag="total", align_bytes=64)
+            nc.scalar.copy(total[:], turned[:])
+            upright = psum.tile([P, n], F32, name="upright", tag="upright", bufs=2)
+            for j in range(blocks):
+                nc.tensor.transpose(upright[:, j * P : (j + 1) * P], total[:, j * P : (j + 1) * P], ident[:])
+            res = ring.tile([P, n], F32, name="res", tag="res", bufs=7, align_bytes=64)
+            nc.scalar.copy(res[:], upright[:])
+            nc.sync.dma_start(out[b * P : (b + 1) * P, t0 : t0 + n], res[:])
+
+        for b in range(3):
+            fill(b + 1)
+            prods = [weighted(b, r, 0, T, f"prod_{r}") for r in range(TOP)]
+            add_on_tensor(b, prods, 0, 0, T // 2)
+            add_on_tensor(b, prods, T // 2, T // 2, T // 2)
+        prods = [weighted(3, r, 0, T - TAIL, f"prod_{r}") for r in range(TOP)]
+        add_on_tensor(3, prods, 0, 0, T - TAIL)
+        last = [weighted(3, r, T - TAIL, TAIL, f"last_{r}") for r in range(2)]
+        pair = held([P, TAIL], F32, "pair")
+        third = weighted(3, 2, T - TAIL, TAIL, "last_2")
+        nc.vector.tensor_tensor(pair[:], last[0][:], last[1][:], ALU.add)
+        res = held([P, TAIL], F32, "res_last")
+        nc.vector.tensor_tensor(res[:], pair[:], third[:], ALU.add)
+        nc.sync.dma_start(out[3 * P : 4 * P, T - TAIL : T], res[:])

@@ -19,8 +19,9 @@ FP8X4 = mybir.dt.float8_e4m3fn_x4
 ACT = mybir.ActivationFunctionType
 ALU = mybir.AluOpType
 
-RELU_ON_VECTOR = [6,7,8,9]
-Y_ON_VECTOR = [1,2]
+RELU_ON_VECTOR = [5,6,7,8,9]
+Y_ON_VECTOR = [3]
+SQUARE_ON_VECTOR = []
 TAIL = 256
 
 
@@ -40,13 +41,21 @@ def tile_moe_cpy_mlp_relu2_kernel(
             return ap.rearrange("p n t -> p (n t)").bitcast(I32)
 
         xs = held([P, T], U8, "xs")
-        w1s = held([P, 2 * H], U8, "w1s")
+        w1s = [keep.tile([P, H], U8, name="w1s_0", tag="odd", align_bytes=64), held([P, H], U8, "w1s_1")]
         w2s = held([P, E * K], U8, "w2s")
         nc.gpsimd.memset(xs[:].bitcast(I32), 0)
-        nc.gpsimd.memset(w1s[:].bitcast(I32), 0)
-        nc.gpsimd.memset(w2s[:].bitcast(I32), 0)
+        nc.gpsimd.memset(w1s[0][:].bitcast(I32), 0)
+        nc.vector.memset(w2s[:].bitcast(I32), 0)
+        nc.gpsimd.memset(w1s[1][:].bitcast(I32), 0)
         zeros = held([P, PAD], F32, "zeros")
         nc.gpsimd.memset(zeros[:], 0.0)
+
+        def load_last_scales(queue):
+            for q in range(4):
+                queue.dma_start(
+                    w1s[1][32 * q : 32 * q + 4, :].bitcast(I32), w1_scales[4, 0, 4 * q : 4 * q + 4, :].bitcast(I32)
+                )
+
         ident = held([P, P], F32, "ident")
         make_identity(nc, ident[:])
 
@@ -56,18 +65,25 @@ def tile_moe_cpy_mlp_relu2_kernel(
         nc.sync.dma_start(xw[:], words(x_words[0]))
         for q in range(4):
             nc.sync.dma_start(xs[32 * q : 32 * q + 4, :].bitcast(I32), x_scales[0, 4 * q : 4 * q + 4, :].bitcast(I32))
-        w1 = [held([P, H], I32, f"w1_{e}") for e in range(E)]
-        nc.sync.dma_start(w1[0][:], words(w1_words[0, 0]))
+        w1 = {}
+
+        def load_w1(a, z):
+            t = held([P, (z - a) * H], I32, f"w1_{a}")
+            nc.sync.dma_start(
+                t[:].rearrange("p (e n) -> p e n", e=z - a),
+                w1_words[a:z, 0].rearrange("e p n t -> p e (n t)").bitcast(I32),
+            )
+            for e in range(a, z):
+                w1[e] = t[:, (e - a) * H : (e - a + 1) * H]
+
+        load_w1(0, 1)
         for q in range(4):
             nc.sync.dma_start(
-                w1s[32 * q : 32 * q + 16, 0:H].bitcast(I32), w1_scales[0:4, 0, 4 * q : 4 * q + 4, :].bitcast(I32)
+                w1s[0][32 * q : 32 * q + 16, :].bitcast(I32), w1_scales[0:4, 0, 4 * q : 4 * q + 4, :].bitcast(I32)
             )
-        for e in range(1, E):
-            nc.sync.dma_start(w1[e][:], words(w1_words[e, 0]))
-        for q in range(4):
-            nc.sync.dma_start(
-                w1s[32 * q : 32 * q + 4, H : 2 * H].bitcast(I32), w1_scales[4, 0, 4 * q : 4 * q + 4, :].bitcast(I32)
-            )
+        load_w1(1, 3)
+        load_w1(3, 5)
+        load_last_scales(nc.sync)
         for q in range(4):
             nc.sync.dma_start(
                 w2s[32 * q : 32 * q + 4, :].bitcast(I32).rearrange("j (e n) -> j e n", e=E),
@@ -106,7 +122,7 @@ def tile_moe_cpy_mlp_relu2_kernel(
                 gw[c // P] = t[:, c - a : c - a + P]
 
         def gather_scales(a, b):
-            t = keep.tile([P, b - a], U8, name="gs", tag="gs", bufs=1, align_bytes=64)
+            t = keep.tile([P, b - a], U8, name="gs", tag="odd" if a == C else "even", align_bytes=64)
             nc.vector.tensor_copy(t[:], xs[:].indirect(slot_list[:, a // 16 : b // 16]))
             for c in range(a, b, P):
                 gs[c // P] = t[:, c - a : c - a + P]
@@ -114,21 +130,22 @@ def tile_moe_cpy_mlp_relu2_kernel(
         def permute_words(e):
             nc.vector.tensor_copy(
                 w1p[e][:].rearrange("p (t c i) -> p c t i", t=4, i=4),
-                w1[e][:].rearrange("p (c i t) -> p c t i", t=4, i=4),
+                w1[e].rearrange("p (c i t) -> p c t i", t=4, i=4),
             )
 
         def permute_scales(c):
             nc.vector.tensor_copy(
                 w1sp[c][:].rearrange("p (t m) -> p t m", t=4),
-                w1s[:, c * H : (c + 1) * H].rearrange("p (m t) -> p t m", t=4),
+                w1s[c][:].rearrange("p (m t) -> p t m", t=4),
             )
 
+        filled = []
         rl = {}
         hb = {}
 
         def first_layer(u):
             e, half = divmod(u, 2)
-            bank = psum.tile([P, 4, P], F32, name="bank", tag="bank", bufs=4)
+            bank = psum.tile([P, 4, P], F32, name="bank", tag=f"bank_{u % 5}")
             row = 4 * (e % 4)
             for t in range(4):
                 nc.tensor.matmul_mx(
@@ -141,8 +158,8 @@ def tile_moe_cpy_mlp_relu2_kernel(
                     stop=True,
                 )
             if half == 0:
-                rl[e] = ring.tile([P, 4 * C], F32, name="rl", align_bytes=64)
-                hb[e] = ring.tile([P, 4 * C], BF16, name="hb", align_bytes=64)
+                rl[e] = ring.tile([P, 4 * C], F32, name="rl", bufs=5, align_bytes=64)
+                hb[e] = ring.tile([P, 4 * C], BF16, name="hb", bufs=5, align_bytes=64)
             dst = rl[e][:, half * 4 * P : (half + 1) * 4 * P].rearrange("p (s t) -> p s t", t=4)
             src = bank[:].rearrange("p t s -> p s t")
             if u in RELU_ON_VECTOR:
@@ -151,30 +168,34 @@ def tile_moe_cpy_mlp_relu2_kernel(
                 nc.scalar.activation(dst, src, ACT.Relu)
 
         def square(e, a, b):
-            nc.scalar.activation(hb[e][:, 4 * a : 4 * b], rl[e][:, 4 * a : 4 * b], ACT.Square)
+            cols = slice(4 * a, 4 * b)
+            if 2 * e + a // P in SQUARE_ON_VECTOR:
+                nc.vector.tensor_tensor(hb[e][:, cols], rl[e][:, cols], rl[e][:, cols], ALU.mult)
+            else:
+                nc.scalar.activation(hb[e][:, cols], rl[e][:, cols], ACT.Square)
 
         def quantise(e, a, b):
             nc.vector.quantize_mx(hq[e][:, a:b].bitcast(FP8X4), hs[e][:, a:b], hb[e][:, 4 * a : 4 * b])
 
-        def second_layer(b, experts, width, on_vector):
-            bank = psum.tile([P, 2 * C], F32, name="ybank", tag="ybank", bufs=2)
-            for j, e in enumerate(experts):
-                for a in range(0, C, width):
-                    nc.tensor.matmul_mx(
-                        bank[:, j * C + a : j * C + a + width],
-                        lhsT=w2[:, e * K + b * P : e * K + (b + 1) * P].bitcast(FP8X4),
-                        lhsT_scale=w2s[:, e * K + b * P : e * K + (b + 1) * P],
-                        rhs=hq[e][:, a : a + width].bitcast(FP8X4),
-                        rhs_scale=hs[e][:, a : a + width],
-                        start=True,
-                        stop=True,
-                    )
-            n = len(experts) * C
-            dst = win[b][:, experts[0] * C : experts[0] * C + n]
+        def second_layer(b, a, n, on_vector):
+            bank = psum.tile([P, n], F32, name="ybank", tag=f"bank_{5 + len(filled) % 3}")
+            filled.append(a)
+            width = min(n, C)
+            for c in range(a, a + n, width):
+                e, u = divmod(c, C)
+                nc.tensor.matmul_mx(
+                    bank[:, c - a : c - a + width],
+                    lhsT=w2[:, e * K + b * P : e * K + (b + 1) * P].bitcast(FP8X4),
+                    lhsT_scale=w2s[:, e * K + b * P : e * K + (b + 1) * P],
+                    rhs=hq[e][:, u : u + width].bitcast(FP8X4),
+                    rhs_scale=hs[e][:, u : u + width],
+                    start=True,
+                    stop=True,
+                )
             if on_vector:
-                nc.vector.tensor_copy(dst, bank[:, 0:n])
+                nc.vector.tensor_copy(win[b][:, a : a + n], bank[:])
             else:
-                nc.scalar.copy(dst, bank[:, 0:n])
+                nc.scalar.copy(win[b][:, a : a + n], bank[:])
 
         gather_words(0, C)
         gather_scales(0, C)
@@ -183,82 +204,83 @@ def tile_moe_cpy_mlp_relu2_kernel(
         permute_scales(0)
         first_layer(0)
         first_layer(1)
-        permute_words(1)
-        permute_words(2)
         gather_scales(C, 3 * C)
+        permute_words(1)
         square(0, 0, C)
         first_layer(2)
         first_layer(3)
         gather_words(2 * C, 4 * C)
-        quantise(0, 0, C)
+        permute_words(2)
         square(1, 0, C)
         first_layer(4)
         first_layer(5)
+        gather_scales(3 * C, S)
         permute_words(3)
         gather_words(4 * C, S)
-        gather_scales(3 * C, S)
-        quantise(1, 0, C)
         permute_words(4)
         permute_scales(1)
         square(2, 0, C)
-        second_layer(0, (0, 1), C, 0 in Y_ON_VECTOR)
         first_layer(6)
         first_layer(7)
-        quantise(2, 0, C)
-        square(3, 0, C)
         first_layer(8)
         first_layer(9)
-        quantise(3, 0, C)
+        square(3, 0, C)
         square(4, 0, P)
         square(4, P, C)
-        second_layer(0, (2, 3), C, 1 in Y_ON_VECTOR)
+        quantise(0, 0, C)
+        quantise(1, 0, C)
+        second_layer(0, 0, 2 * C, 0 in Y_ON_VECTOR)
+        quantise(2, 0, C)
+        quantise(3, 0, C)
+        second_layer(0, 2 * C, 2 * C, 1 in Y_ON_VECTOR)
         quantise(4, 0, P)
+        second_layer(0, 4 * C, P, 2 in Y_ON_VECTOR)
         quantise(4, P, C)
-        second_layer(0, (4,), P, 2 in Y_ON_VECTOR)
+        second_layer(0, 4 * C + P, P, 3 in Y_ON_VECTOR)
 
         def fill(b):
-            for experts in ((0, 1), (2, 3), (4,)):
-                second_layer(b, experts, C, False)
+            for a in range(0, S, 2 * C):
+                second_layer(b, a, min(2 * C, S - a), False)
 
         def weighted(b, r, a, n, tag):
-            prod = ring.tile([P, n], F32, name=tag, tag=tag, align_bytes=64)
+            prod = ring.tile([P, n], F32, name=tag, tag=tag, bufs=3, align_bytes=64)
             nc.vector.tensor_tensor(
                 prod[:], win[b][:].indirect(back[r][:, a // 16 : (a + n) // 16]), g[:, r * T + a : r * T + a + n], ALU.mult
             )
             return prod
 
-        def add_on_tensor(b, prods, a, t0, n):
-            blocks = n // P
-            turned = psum.tile([P, n], F32, name="turned", tag="bank", bufs=4)
+        def add_on_tensor(b, tokens):
+            n = tokens // 2 if tokens > T // 2 else tokens
+            turned = [psum.tile([P, n], F32, name="turned", tag=f"bank_{6 + a // n}") for a in range(0, tokens, n)]
             for r in range(TOP):
-                for j in range(blocks):
+                prod = weighted(b, r, 0, tokens, f"prod_{r}")
+                for c in range(0, tokens, P):
                     nc.tensor.matmul(
-                        turned[:, j * P : (j + 1) * P],
-                        prods[r][:, a + j * P : a + (j + 1) * P],
+                        turned[c // n][:, c % n : c % n + P],
+                        prod[:, c : c + P],
                         ident[:],
-                        start=(r == 0 and j == 0),
-                        stop=(r == TOP - 1 and j == blocks - 1),
+                        start=(r == 0 and c % n == 0),
+                        stop=(r == TOP - 1 and c % n == n - P),
                         is_transpose=True,
                     )
-            total = ring.tile([P, n], F32, name="total", tag="total", align_bytes=64)
-            nc.scalar.copy(total[:], turned[:])
-            upright = psum.tile([P, n], F32, name="upright", tag="upright", bufs=2)
-            for j in range(blocks):
-                nc.tensor.transpose(upright[:, j * P : (j + 1) * P], total[:, j * P : (j + 1) * P], ident[:])
-            res = ring.tile([P, n], F32, name="res", tag="res", bufs=7, align_bytes=64)
-            nc.scalar.copy(res[:], upright[:])
-            nc.sync.dma_start(out[b * P : (b + 1) * P, t0 : t0 + n], res[:])
+            for a in range(0, tokens, n):
+                total = ring.tile([P, n], F32, name="total", tag="total", align_bytes=64)
+                nc.scalar.copy(total[:], turned[a // n][:])
+                upright = psum.tile([P, n], F32, name="upright", tag=f"bank_{a // n}")
+                for c in range(0, n, P):
+                    nc.tensor.transpose(upright[:, c : c + P], total[:, c : c + P], ident[:])
+                res = ring.tile([P, n], F32, name="res", tag="res", bufs=7, align_bytes=64)
+                nc.scalar.copy(res[:], upright[:])
+                nc.scalar.dma_start(out[b * P : (b + 1) * P, a : a + n], res[:])
 
+        for b in range(1, 4):
+            fill(b)
         for b in range(3):
-            fill(b + 1)
-            prods = [weighted(b, r, 0, T, f"prod_{r}") for r in range(TOP)]
-            add_on_tensor(b, prods, 0, 0, T // 2)
-            add_on_tensor(b, prods, T // 2, T // 2, T // 2)
-        prods = [weighted(3, r, 0, T - TAIL, f"prod_{r}") for r in range(TOP)]
-        add_on_tensor(3, prods, 0, 0, T - TAIL)
-        last = [weighted(3, r, T - TAIL, TAIL, f"last_{r}") for r in range(2)]
+            add_on_tensor(b, T)
+        add_on_tensor(3, T - TAIL)
+        last = [weighted(3, r, T - TAIL, TAIL, f"prod_{r}") for r in range(2)]
         pair = held([P, TAIL], F32, "pair")
-        third = weighted(3, 2, T - TAIL, TAIL, "last_2")
+        third = weighted(3, 2, T - TAIL, TAIL, "prod_2")
         nc.vector.tensor_tensor(pair[:], last[0][:], last[1][:], ALU.add)
         res = held([P, TAIL], F32, "res_last")
         nc.vector.tensor_tensor(res[:], pair[:], third[:], ALU.add)

from contextlib import ExitStack

import concourse.mybir as mybir
from concourse.masks import make_identity

K, T, E, C, H, TOP, PAD = 512, 768, 5, 256, 512, 3, 64
S = E * C
W = S + T + PAD
P = 128
FLOPS = 2 * S * K * H * 2

F32 = mybir.dt.float32
BF16 = mybir.dt.bfloat16
I32 = mybir.dt.int32
U32 = mybir.dt.uint32
U16 = mybir.dt.uint16
U8 = mybir.dt.uint8
FP8X4 = mybir.dt.float8_e4m3fn_x4
ACT = mybir.ActivationFunctionType
ALU = mybir.AluOpType

RELU_ON_VECTOR = [5,6,7,8,9]
Y_ON_VECTOR = [3]
SQUARE_ON_VECTOR = []
TAIL = 256


def tile_moe_cpy_mlp_relu2_kernel(
    tc, x_words, x_scales, xr, w1_words, w1_scales, w2_words, w2_scales, gate, offs, pos1, pos2, pos3, out
):
    nc = tc.nc
    with ExitStack() as ctx:
        keep = ctx.enter_context(tc.tile_pool(name="keep", bufs=1))
        ring = ctx.enter_context(tc.tile_pool(name="ring", bufs=2))
        psum = ctx.enter_context(tc.psum_pool(name="psum", bufs=1))

        def held(shape, dtype, name):
            return keep.tile(shape, dtype, name=name, align_bytes=64)

        def words(ap):
            return ap.rearrange("p n t -> p (n t)").bitcast(I32)

        xs = held([P, T], U8, "xs")
        w1s = [keep.tile([P, H], U8, name="w1s_0", tag="odd", align_bytes=64), held([P, H], U8, "w1s_1")]
        w2s = held([P, E * K], U8, "w2s")
        nc.gpsimd.memset(xs[:].bitcast(I32), 0)
        nc.gpsimd.memset(w1s[0][:].bitcast(I32), 0)
        nc.vector.memset(w2s[:].bitcast(I32), 0)
        nc.gpsimd.memset(w1s[1][:].bitcast(I32), 0)
        zeros = held([P, PAD], F32, "zeros")
        nc.gpsimd.memset(zeros[:], 0.0)

        def load_last_scales(queue):
            for q in range(4):
                queue.dma_start(
                    w1s[1][32 * q : 32 * q + 4, :].bitcast(I32), w1_scales[4, 0, 4 * q : 4 * q + 4, :].bitcast(I32)
                )

        ident = held([P, P], F32, "ident")
        make_identity(nc, ident[:])

        slot_list = held([P, S // 16], U16, "slot_list")
        nc.sync.dma_start(slot_list[:], offs)
        xw = held([P, T], I32, "xw")
        nc.sync.dma_start(xw[:], words(x_words[0]))
        for q in range(4):
            nc.sync.dma_start(xs[32 * q : 32 * q + 4, :].bitcast(I32), x_scales[0, 4 * q : 4 * q + 4, :].bitcast(I32))
        w1 = {}

        def load_w1(a, z):
            t = held([P, (z - a) * H], I32, f"w1_{a}")
            nc.sync.dma_start(
                t[:].rearrange("p (e n) -> p e n", e=z - a),
                w1_words[a:z, 0].rearrange("e p n t -> p e (n t)").bitcast(I32),
            )
            for e in range(a, z):
                w1[e] = t[:, (e - a) * H : (e - a + 1) * H]

        load_w1(0, 1)
        for q in range(4):
            nc.sync.dma_start(
                w1s[0][32 * q : 32 * q + 16, :].bitcast(I32), w1_scales[0:4, 0, 4 * q : 4 * q + 4, :].bitcast(I32)
            )
        load_w1(1, 3)
        load_w1(3, 5)
        load_last_scales(nc.sync)
        for q in range(4):
            nc.sync.dma_start(
                w2s[32 * q : 32 * q + 4, :].bitcast(I32).rearrange("j (e n) -> j e n", e=E),
                w2_scales[:, 0, 4 * q : 4 * q + 4, :].bitcast(I32).rearrange("e j n -> j e n"),
            )
        w2 = held([P, E * K], I32, "w2")
        nc.sync.dma_start(
            w2[:].rearrange("p (e n) -> p e n", e=E),
            w2_words[:, 0].rearrange("e p n t -> p e (n t)").bitcast(I32),
        )
        win = [held([P, W], F32, f"win_{b}") for b in range(4)]
        nc.sync.dma_start(win[0][:, S : S + T], xr[0:P, :])
        back = []
        for r, lst in enumerate((pos1, pos2, pos3)):
            t = held([P, T // 16], U16, f"back_{r}")
            nc.sync.dma_start(t[:], lst)
            back.append(t)
        g = held([P, TOP * T], F32, "g")
        nc.sync.dma_start(g[:].rearrange("p (r t) -> p r t", r=TOP), gate.rearrange("r p t -> p r t"))
        for b in range(1, 4):
            nc.sync.dma_start(win[b][:, S : S + T], xr[b * P : (b + 1) * P, :])
        for b in range(4):
            nc.scalar.activation(win[b][:, S + T : W], zeros[:], ACT.Relu)

        gw = {}
        gs = {}
        w1p = [held([P, H], I32, f"w1p_{e}") for e in range(E)]
        w1sp = [held([P, H], U8, f"w1sp_{c}") for c in range(2)]
        hq = [held([P, C], U32, f"hq_{e}") for e in range(E)]
        hs = [held([P, C], U8, f"hs_{e}") for e in range(E)]

        def gather_words(a, b):
            t = keep.tile([P, b - a], U32, name="gw", tag="gw", bufs=2, align_bytes=64)
            nc.vector.tensor_copy(t[:], xw[:].bitcast(U32).indirect(slot_list[:, a // 16 : b // 16]))
            for c in range(a, b, P):
                gw[c // P] = t[:, c - a : c - a + P]

        def gather_scales(a, b):
            t = keep.tile([P, b - a], U8, name="gs", tag="odd" if a == C else "even", align_bytes=64)
            nc.vector.tensor_copy(t[:], xs[:].indirect(slot_list[:, a // 16 : b // 16]))
            for c in range(a, b, P):
                gs[c // P] = t[:, c - a : c - a + P]

        def permute_words(e):
            nc.vector.tensor_copy(
                w1p[e][:].rearrange("p (t c i) -> p c t i", t=4, i=4),
                w1[e].rearrange("p (c i t) -> p c t i", t=4, i=4),
            )

        def permute_scales(c):
            nc.vector.tensor_copy(
                w1sp[c][:].rearrange("p (t m) -> p t m", t=4),
                w1s[c][:].rearrange("p (m t) -> p t m", t=4),
            )

        filled = []
        rl = {}
        hb = {}

        def first_layer(u):
            e, half = divmod(u, 2)
            bank = psum.tile([P, 4, P], F32, name="bank", tag=f"bank_{u % 5}")
            row = 4 * (e % 4)
            for t in range(4):
                nc.tensor.matmul_mx(
                    bank[:, t, :],
                    lhsT=w1p[e][:, t * P : (t + 1) * P].bitcast(FP8X4),
                    lhsT_scale=w1sp[e // 4][row:P, t * P : (t + 1) * P],
                    rhs=gw[u].bitcast(FP8X4),
                    rhs_scale=gs[u],
                    start=True,
                    stop=True,
                )
            if half == 0:
                rl[e] = ring.tile([P, 4 * C], F32, name="rl", bufs=5, align_bytes=64)
                hb[e] = ring.tile([P, 4 * C], BF16, name="hb", bufs=5, align_bytes=64)
            dst = rl[e][:, half * 4 * P : (half + 1) * 4 * P].rearrange("p (s t) -> p s t", t=4)
            src = bank[:].rearrange("p t s -> p s t")
            if u in RELU_ON_VECTOR:
                nc.vector.tensor_scalar(dst, src, 0.0, None, ALU.max)
            else:
                nc.scalar.activation(dst, src, ACT.Relu)

        def square(e, a, b):
            cols = slice(4 * a, 4 * b)
            if 2 * e + a // P in SQUARE_ON_VECTOR:
                nc.vector.tensor_tensor(hb[e][:, cols], rl[e][:, cols], rl[e][:, cols], ALU.mult)
            else:
                nc.scalar.activation(hb[e][:, cols], rl[e][:, cols], ACT.Square)

        def quantise(e, a, b):
            nc.vector.quantize_mx(hq[e][:, a:b].bitcast(FP8X4), hs[e][:, a:b], hb[e][:, 4 * a : 4 * b])

        def second_layer(b, a, n, on_vector):
            bank = psum.tile([P, n], F32, name="ybank", tag=f"bank_{5 + len(filled) % 3}")
            filled.append(a)
            width = min(n, C)
            for c in range(a, a + n, width):
                e, u = divmod(c, C)
                nc.tensor.matmul_mx(
                    bank[:, c - a : c - a + width],
                    lhsT=w2[:, e * K + b * P : e * K + (b + 1) * P].bitcast(FP8X4),
                    lhsT_scale=w2s[:, e * K + b * P : e * K + (b + 1) * P],
                    rhs=hq[e][:, u : u + width].bitcast(FP8X4),
                    rhs_scale=hs[e][:, u : u + width],
                    start=True,
                    stop=True,
                )
            if on_vector:
                nc.vector.tensor_copy(win[b][:, a : a + n], bank[:])
            else:
                nc.scalar.copy(win[b][:, a : a + n], bank[:])

        gather_words(0, C)
        gather_scales(0, C)
        permute_words(0)
        gather_words(C, 2 * C)
        permute_scales(0)
        first_layer(0)
        first_layer(1)
        gather_scales(C, 3 * C)
        permute_words(1)
        square(0, 0, C)
        first_layer(2)
        first_layer(3)
        gather_words(2 * C, 4 * C)
        permute_words(2)
        square(1, 0, C)
        first_layer(4)
        first_layer(5)
        gather_scales(3 * C, S)
        permute_words(3)
        gather_words(4 * C, S)
        permute_words(4)
        permute_scales(1)
        square(2, 0, C)
        first_layer(6)
        first_layer(7)
        first_layer(8)
        first_layer(9)
        square(3, 0, C)
        square(4, 0, P)
        square(4, P, C)
        quantise(0, 0, C)
        quantise(1, 0, C)
        second_layer(0, 0, 2 * C, 0 in Y_ON_VECTOR)
        quantise(2, 0, C)
        quantise(3, 0, C)
        second_layer(0, 2 * C, 2 * C, 1 in Y_ON_VECTOR)
        quantise(4, 0, P)
        second_layer(0, 4 * C, P, 2 in Y_ON_VECTOR)
        quantise(4, P, C)
        second_layer(0, 4 * C + P, P, 3 in Y_ON_VECTOR)

        def fill(b):
            for a in range(0, S, 2 * C):
                second_layer(b, a, min(2 * C, S - a), False)

        def weighted(b, r, a, n, tag):
            prod = ring.tile([P, n], F32, name=tag, tag=tag, bufs=3, align_bytes=64)
            nc.vector.tensor_tensor(
                prod[:], win[b][:].indirect(back[r][:, a // 16 : (a + n) // 16]), g[:, r * T + a : r * T + a + n], ALU.mult
            )
            return prod

        def add_on_tensor(b, tokens):
            n = tokens // 2 if tokens > T // 2 else tokens
            turned = [psum.tile([P, n], F32, name="turned", tag=f"bank_{6 + a // n}") for a in range(0, tokens, n)]
            for r in range(TOP):
                prod = weighted(b, r, 0, tokens, f"prod_{r}")
                for c in range(0, tokens, P):
                    nc.tensor.matmul(
                        turned[c // n][:, c % n : c % n + P],
                        prod[:, c : c + P],
                        ident[:],
                        start=(r == 0 and c % n == 0),
                        stop=(r == TOP - 1 and c % n == n - P),
                        is_transpose=True,
                    )
            for a in range(0, tokens, n):
                total = ring.tile([P, n], F32, name="total", tag="total", align_bytes=64)
                nc.scalar.copy(total[:], turned[a // n][:])
                upright = psum.tile([P, n], F32, name="upright", tag=f"bank_{a // n}")
                for c in range(0, n, P):
                    nc.tensor.transpose(upright[:, c : c + P], total[:, c : c + P], ident[:])
                res = ring.tile([P, n], F32, name="res", tag="res", bufs=7, align_bytes=64)
                nc.scalar.copy(res[:], upright[:])
                nc.scalar.dma_start(out[b * P : (b + 1) * P, a : a + n], res[:])

        for b in range(1, 4):
            fill(b)
        for b in range(3):
            add_on_tensor(b, T)
        add_on_tensor(3, T - TAIL)
        last = [weighted(3, r, T - TAIL, TAIL, f"prod_{r}") for r in range(2)]
        pair = held([P, TAIL], F32, "pair")
        third = weighted(3, 2, T - TAIL, TAIL, "prod_2")
        nc.vector.tensor_tensor(pair[:], last[0][:], last[1][:], ALU.add)
        res = held([P, TAIL], F32, "res_last")
        nc.vector.tensor_tensor(res[:], pair[:], third[:], ALU.add)
        nc.sync.dma_start(out[3 * P : 4 * P, T - TAIL : T], res[:])
